import numpy as np
import ml_dtypes


def mxq(x, axis, fmt="e4m3"):
    dtype, down = {"e4m3": (ml_dtypes.float8_e4m3fn, 7), "e5m2": (ml_dtypes.float8_e5m2, 14)}[fmt]
    v = np.moveaxis(np.asarray(x, np.float32).astype(ml_dtypes.bfloat16).astype(np.float64), axis, -1)
    blocks = v.reshape(v.shape[:-1] + (-1, 32))
    amax = np.abs(blocks).max(-1, keepdims=True)
    byte = np.maximum(np.where(amax > 0, np.frexp(amax)[1] - 1 + 127, 0) - down, 1)
    scale = np.exp2(byte - 127.0)
    codes = (blocks / scale).astype(np.float32).astype(dtype).astype(np.float64)
    return np.moveaxis((codes * scale).reshape(v.shape), -1, axis)


WIDE = False


def mx_kscale(k):
    if not WIDE:
        return np.ones(k)
    levels = np.array([10, -10, 5, -5, 0])
    if k % 512:
        return np.exp2(np.random.permutation(np.resize(levels, k // 32))).repeat(32)
    a = np.empty((k // 512, 16))
    for p in range(k // 512):
        a[p, :8] = np.random.permutation(np.resize(levels, 8))
        for g in range(8):
            far = levels[np.abs(levels - a[p, g]) >= 10]
            a[p, g + 8] = far[np.random.randint(len(far))]
    return np.exp2(a.ravel()).repeat(32)


BF16 = ml_dtypes.bfloat16


def bf(x):
    return np.asarray(x, np.float32).astype(BF16)


def f64(x):
    return np.asarray(x).astype(np.float64)


B, L, R, D = 8, 1024, 2, 128


def time_gain(g, z):
    return g[None, :, None] * z


def time_mix(m, z):
    return mxq(m, 1, "e4m3") @ mxq(z, 1, "e4m3")


def draw0():
    s, u = mx_kscale(L), mx_kscale(L)
    root = np.sqrt(L)
    return {
        "x": bf(np.random.standard_normal((B, L, R, D))),
        "g1": bf((1.0 + 0.1 * np.random.standard_normal(L)) * s),
        "ma": bf(np.random.standard_normal((L, L)) / root / s[None, :]),
        "mc": bf(np.random.standard_normal((L, L)) / root / s[None, :]),
        "g2": bf((1.0 + 0.1 * np.random.standard_normal(L)) * u),
        "mu": bf(np.random.standard_normal((L, L)) / root / u[None, :]),
        "mv": bf(np.random.standard_normal((L, L)) / root / u[None, :]),
    }


def core(x, g1, ma, mc, g2, mu, mv):
    x = f64(x)
    g1, g2 = f64(g1), f64(g2)

    e = x[:, :, 0, :]
    o = x[:, :, 1, :]

    eg = time_gain(g1, e)
    og = time_gain(g1, o)

    pa = time_mix(f64(ma), og)
    pc = time_mix(f64(mc), eg)

    e1 = e * np.exp(np.tanh(pa))
    o1 = o * np.exp(np.tanh(pc))

    e1g = time_gain(g2, e1)
    o1g = time_gain(g2, o1)

    pu = time_mix(f64(mu), o1g)
    pv = time_mix(f64(mv), e1g)

    e2 = e1 + np.tanh(pu)
    o2 = o1 - np.tanh(pv)
    return e2, o2


def e4m3fn_bytes(y):
    return np.clip(np.asarray(y, np.float64), -448.0, 448.0).astype(np.float32).astype(ml_dtypes.float8_e4m3fn).view(np.uint8)


def e4m3fn_values(b):
    return np.asarray(b, np.uint8).view(ml_dtypes.float8_e4m3fn).astype(np.float64)


def setup_inputs():
    d = draw0()
    x0 = np.asarray(d['mv']).astype(np.float64)
    s = (np.max(np.abs(x0), axis=(0,), keepdims=True) / 448.0).astype(np.float32)
    out = {}
    for k, v in d.items():
        if k == 'mv':
            out['mv_bytes'] = e4m3fn_bytes(x0 / s.astype(np.float64))
            out['mv_scale'] = s
        else:
            out[k] = v
    return out


def reference(x, g1, ma, mc, g2, mu, mv_bytes, mv_scale):
    return core(x, g1, ma, mc, g2, mu, e4m3fn_values(mv_bytes) * mv_scale.astype(np.float64))

from contextlib import ExitStack

import concourse.mybir as mybir
from concourse.masks import make_identity

B, L, D = 8, 1024, 128
P = 128
N_CHUNKS = 4
FLOPS = 4 * 2 * L * L * B * D

F32 = mybir.dt.float32
BF16 = mybir.dt.bfloat16
U32 = mybir.dt.uint32
U8 = mybir.dt.uint8
FP8 = mybir.dt.float8_e4m3fn
FP8X4 = mybir.dt.float8_e4m3fn_x4
ACT = mybir.ActivationFunctionType
ALU = mybir.AluOpType

MODE = {(u, h): ("P" if h == 0 else ("S" if u in (1, 3, 5, 6, 7) else "V")) for u in range(8) for h in range(2)}


def tile_scinetevenoddinteraction_t_kernel(tc, x, g1, ma, mc, g2, mu, mv_bytes, mv_scale, out_0, out_1):
    nc = tc.nc
    with ExitStack() as ctx:
        keep = ctx.enter_context(tc.tile_pool(name="keep", bufs=1))
        rawp = ctx.enter_context(tc.tile_pool(name="rawp", bufs=6))
        two = ctx.enter_context(tc.tile_pool(name="two", bufs=2))
        three = ctx.enter_context(tc.tile_pool(name="three", bufs=3))
        five = ctx.enter_context(tc.tile_pool(name="five", bufs=5))
        ten = ctx.enter_context(tc.tile_pool(name="ten", bufs=10))
        psum = ctx.enter_context(tc.psum_pool(name="psum", bufs=4))

        ident32 = keep.tile([P, P], F32, name="ident32")
        make_identity(nc, ident32[:])
        ident16 = keep.tile([P, P], BF16, name="ident16")
        make_identity(nc, ident16[:])
        warm = keep.tile([P, 1], F32, name="warm")
        nc.gpsimd.memset(warm[:], 0.0)
        nc.scalar.activation(out=warm[:], in_=warm[:], func=ACT.Tanh)

        g1t = keep.tile([P, 2, 1, 4], BF16, name="g1t")
        g2t = keep.tile([P, 2, 1, 4], BF16, name="g2t")
        scale = keep.tile([P, L], F32, name="scale")
        xts = [keep.tile([P, 2, 2, 1024], BF16, name=f"x{c}") for c in range(N_CHUNKS)]
        xv = [t[:].rearrange("p b g (t r d) -> p b g t r d", t=4, r=2) for t in xts]
        names = ("ma", "mc", "mu", "mv")
        wcodes = {n: keep.tile([P, 2048], U32, name=f"wc_{n}", align_bytes=64) for n in names}
        wscales = {n: keep.tile([P, 2048], U8, name=f"ws_{n}", align_bytes=64) for n in names}
        hbm = {"ma": ma, "mc": mc, "mu": mu}
        raws = {}

        def load_w(n, q):
            t = rawp.tile([P, 2, 1024], BF16, name="raw")
            nc.sync.dma_start(
                out=t[:].rearrange("p a k -> p (a k)"),
                in_=hbm[n].rearrange("(q0 m q1 a) k -> q0 q1 m (a k)", q0=2, q1=2, a=2)[q // 2, q % 2],
            )
            raws[n, q] = t

        def load_mv(h):
            t = two.tile([P, 4, 1024], U8, name="mvb")
            nc.sync.dma_start(
                out=t[:].rearrange("p a k -> p (a k)"),
                in_=mv_bytes.rearrange("(h m a) k -> h m (a k)", h=2, a=4)[h],
            )
            raws["mvb", h] = t

        def load_x(c):
            for b in range(2):
                nc.sync.dma_start(
                    out=xts[c][:, b],
                    in_=x[2 * c + b].rearrange("(g p t) r d -> p g (t r d)", g=2, t=4),
                )

        def load_g(t, g):
            nc.sync.dma_start(out=t[:].rearrange("p g o t -> p g (o t)"), in_=g.rearrange("(g p t) -> p g t", g=2, t=4))

        load_w("ma", 0)
        load_w("ma", 1)
        load_g(g1t, g1)
        load_x(0)
        load_w("ma", 2)
        load_w("ma", 3)
        for q in range(4):
            load_w("mc", q)
        load_g(g2t, g2)
        load_x(1)
        for q in range(4):
            load_w("mu", q)
        nc.sync.dma_start(out=scale[:], in_=mv_scale.rearrange("o k -> (o k)").partition_broadcast(P))
        load_mv(0)
        load_mv(1)
        load_x(2)
        load_x(3)

        def prod_mv(q):
            t = two.tile([P, 2, 1024], BF16, name="mvs")
            for a in range(2):
                nc.vector.tensor_tensor(
                    out=t[:, a, :],
                    in0=raws["mvb", q // 2][:, 2 * (q % 2) + a, :].bitcast(FP8),
                    in1=scale[:],
                    op=ALU.mult,
                )
            raws["mv", q] = t

        def weights(n, q, engines):
            raw = raws[n, q]
            wt = three.tile([P, 2, 1024], BF16, name="wt", align_bytes=64)
            for a in range(2):
                words = raw[:, a, :].bitcast(F32)
                pt = psum.tile([P, 4, P], F32, name="pt", tag="aux")
                for g in range(2):
                    for e in range(2):
                        nc.tensor.transpose(pt[:, 2 * g + e, :], words[:, 256 * g + e : 256 * (g + 1) : 2], ident32[:])
                dst = wt[:, a, :].bitcast(F32).rearrange("p (g m e) -> p g m e", g=2, e=2)
                src = pt[:].rearrange("p (g e) m -> p g m e", g=2)
                if engines[a] == "V":
                    nc.vector.tensor_copy(out=dst, in_=src)
                else:
                    nc.scalar.copy(out=dst, in_=src)
            cols = slice(512 * q, 512 * (q + 1))
            nc.vector.quantize_mx(
                out=wcodes[n][:, cols].bitcast(FP8X4),
                scales=wscales[n][:, cols],
                in_=wt[:].rearrange("p a k -> p (a k)"),
            )

        ops1, ops2, firsts = {}, {}, {}

        def stage_a(u):
            c, r = u // 2, 1 - u % 2
            xg = two.tile([P, 2, 1024], BF16, name="xg", align_bytes=64)
            for g in range(2):
                bank = psum.tile([P, 2, 512], BF16, name="bank", tag="aux")
                for b in range(2):
                    nc.tensor.matmul(
                        out=bank[:, b, :].rearrange("p (d t) -> p d t", t=4),
                        lhsT=ident16[:],
                        rhs=xv[c][:, b, g, :, r, :].rearrange("p t d -> p d t"),
                        start=True,
                        stop=True,
                    )
                nc.vector.tensor_tensor(
                    out=xg[:, g, :].rearrange("p (n t) -> p n t", t=4),
                    in0=bank[:].rearrange("p b (d t) -> p (b d) t", t=4),
                    in1=g1t[:, g, :, :].to_broadcast([P, 256, 4]),
                    op=ALU.mult,
                )
            codes = three.tile([P, 512], U32, name="xc", align_bytes=64)
            scales = three.tile([P, 512], U8, name="xs", align_bytes=64)
            nc.vector.quantize_mx(out=codes[:].bitcast(FP8X4), scales=scales[:], in_=xg[:].rearrange("p g n -> p (g n)"))
            ops1[u] = (codes, scales)

        def product(n, q, operand):
            codes, scales = operand
            acc = psum.tile([P, 2, 256], F32, name="acc", tag="mx")
            for a in range(2):
                for g in range(2):
                    w = 512 * q + 256 * a + 128 * g
                    nc.tensor.matmul_mx(
                        out=acc[:, a, :],
                        lhsT=wcodes[n][:, w : w + 128].bitcast(FP8X4),
                        lhsT_scale=wscales[n][:, w : w + 128],
                        rhs=codes[:, 256 * g : 256 * (g + 1)].bitcast(FP8X4),
                        rhs_scale=scales[:, 256 * g : 256 * (g + 1)],
                        start=(g == 0),
                        stop=(g == 1),
                    )
            return acc

        def tanh_out(acc, th, q):
            jp = q % 2
            nc.scalar.activation(
                out=th[:, :, 2 * jp : 2 * jp + 2, :].rearrange("p b j d -> p j b d"),
                in_=acc[:].rearrange("p j (b d) -> p j b d", b=2),
                func=ACT.Tanh,
            )

        ths = {}

        def stage_b(u, q):
            h = q // 2
            if q % 2 == 0:
                ths[u, h] = five.tile([P, 2, 4, P], F32, name="th")
            acc = product("ma" if u % 2 == 0 else "mc", q, ops1[u])
            tanh_out(acc, ths[u, h], q)
            if q % 2 == 1:
                flat = ths[u, h][:].rearrange("p b j d -> p (b j d)")
                nc.scalar.activation(out=flat, in_=flat, func=ACT.Exp)

        eis = {}

        def stage_c(u, h):
            c, r = u // 2, u % 2
            f = ten.tile([P, 2, 4, P], F32, name="f")
            nc.vector.tensor_tensor(out=f[:], in0=ths[u, h][:], in1=xv[c][:, :, h, :, r, :], op=ALU.mult)
            firsts[u, h] = f
            if h == 0:
                eis[u] = two.tile([P, 2, 1024], BF16, name="ei", align_bytes=64)
            ei = eis[u]
            mode = MODE[u, h]
            if mode == "V":
                nc.vector.tensor_tensor(
                    out=ei[:, h, :].rearrange("p (b d j) -> p b d j", b=2, j=4),
                    in0=f[:].rearrange("p b j d -> p b d j"),
                    in1=g2t[:, h : h + 1, :, :].to_broadcast([P, 2, P, 4]),
                    op=ALU.mult,
                )
            else:
                fg = three.tile([P, 2, 4, P], BF16, name="fg")
                for j in range(4):
                    nc.vector.tensor_scalar(
                        out=fg[:, :, j, :], in0=f[:, :, j, :], scalar1=g2t[:, h, 0, j : j + 1], scalar2=None, op0=ALU.mult
                    )
                if mode == "P":
                    bank = psum.tile([P, 2, 512], BF16, name="bank", tag="aux")
                    for b in range(2):
                        nc.tensor.matmul(
                            out=bank[:, b, :].rearrange("p (d t) -> p d t", t=4),
                            lhsT=ident16[:],
                            rhs=fg[:, b, :, :].rearrange("p j d -> p d j"),
                            start=True,
                            stop=True,
                        )
                    nc.scalar.copy(out=ei[:, h, :], in_=bank[:].rearrange("p b n -> p (b n)"))
                else:
                    nc.scalar.copy(
                        out=ei[:, h, :].rearrange("p (b d j) -> p b d j", b=2, j=4),
                        in_=fg[:].rearrange("p b j d -> p b d j"),
                    )
            if h == 1:
                codes = three.tile([P, 512], U32, name="ec", align_bytes=64)
                scales = three.tile([P, 512], U8, name="es", align_bytes=64)
                nc.vector.quantize_mx(out=codes[:].bitcast(FP8X4), scales=scales[:], in_=ei[:].rearrange("p g n -> p (g n)"))
                ops2[u] = (codes, scales)

        def stage_d(u, h):
            th = five.tile([P, 2, 4, P], F32, name="th")
            for q in (2 * h, 2 * h + 1):
                acc = product("mv" if u % 2 == 0 else "mu", q, ops2[u])
                tanh_out(acc, th, q)
            f = firsts[u ^ 1, h]
            out = out_1 if u % 2 == 0 else out_0
            nc.vector.tensor_tensor(out=f[:], in0=f[:], in1=th[:], op=ALU.subtract if u % 2 == 0 else ALU.add)
            c = u // 2
            nc.sync.dma_start(
                out=out.rearrange("b (h p j) d -> h p b (j d)", h=2, j=4)[h][:, 2 * c : 2 * c + 2, :],
                in_=f[:].rearrange("p b j d -> p b (j d)"),
            )

        weights("ma", 0, "VS")
        weights("ma", 1, "VS")
        stage_a(0)
        stage_b(0, 0)
        weights("ma", 2, "VS")
        stage_b(0, 1)
        weights("ma", 3, "SS")
        stage_a(1)
        for q in range(4):
            weights("mc", q, "SS")
            if q < 2:
                stage_b(0, q + 2)
            else:
                stage_c(0, q - 2)
        for q in range(4):
            stage_b(1, q)
            weights("mu", q, "SS")
        stage_a(2)
        second = {2: (1,), 3: (0,), 4: (3,), 5: (2, 4), 6: (5,), 7: (6,), 8: (7,)}
        for k in range(1, 9):
            if 3 <= k + 2 < 8:
                stage_a(k + 2)
            for h in range(2):
                if k + 1 < 8:
                    stage_b(k + 1, 2 * h)
                    stage_b(k + 1, 2 * h + 1)
                if k < 8:
                    stage_c(k, h)
                for d in second.get(k, ()):
                    stage_d(d, h)
                if k in (1, 2):
                    q = 2 * (k - 1) + h
                    prod_mv(q)
                    weights("mv", q, "SS")
